import numpy as np
import ml_dtypes


def mxq(x, axis, fmt="e4m3"):
    dtype, down = {"e4m3": (ml_dtypes.float8_e4m3fn, 7), "e5m2": (ml_dtypes.float8_e5m2, 14)}[fmt]
    v = np.moveaxis(np.asarray(x, np.float32).astype(ml_dtypes.bfloat16).astype(np.float64), axis, -1)
    blocks = v.reshape(v.shape[:-1] + (-1, 32))
    amax = np.abs(blocks).max(-1, keepdims=True)
    byte = np.maximum(np.where(amax > 0, np.frexp(amax)[1] - 1 + 127, 0) - down, 1)
    scale = np.exp2(byte - 127.0)
    codes = (blocks / scale).astype(np.float32).astype(dtype).astype(np.float64)
    return np.moveaxis((codes * scale).reshape(v.shape), -1, axis)


WIDE = False


def mx_kscale(k):
    if not WIDE:
        return np.ones(k)
    levels = np.array([30, -30])
    if k % 512:
        return np.exp2(np.random.permutation(np.resize(levels, k // 32))).repeat(32)
    a = np.empty((k // 512, 16))
    for p in range(k // 512):
        a[p, :8] = np.random.permutation(np.resize(levels, 8))
        for g in range(8):
            far = levels[np.abs(levels - a[p, g]) >= 10]
            a[p, g + 8] = far[np.random.randint(len(far))]
    return np.exp2(a.ravel()).repeat(32)


def f64(x):
    return np.asarray(x).astype(np.float64)


def striped(idx):
    return np.tile(np.asarray(idx).reshape(-1, 16).T, (8, 1)).astype(np.uint16)


def unstriped(offs):
    return offs[:16].T.reshape(-1).astype(np.int64)


E2M1 = np.array([0.0, 0.5, 1.0, 1.5, 2.0, 3.0, 4.0, 6.0, -0.0, -0.5, -1.0, -1.5, -2.0, -3.0, -4.0, -6.0])


def pack_weight(w, fmt):
    k, n = w.shape
    w = f64(np.asarray(w, np.float32).astype(ml_dtypes.bfloat16)).reshape(k // 32, 32, n)
    amax = np.abs(w).max(1)
    if fmt in ("e4m3", "e5m2"):
        byte = np.frexp(amax)[1] - 1 + 127 - (7 if fmt == "e4m3" else 14)
    else:
        mant, ex = np.frexp(amax / 6.0)
        byte = np.where(mant > 0.5, ex, ex - 1) + 127
    byte = np.clip(np.where(amax > 0, byte, 1), 1, 254)
    scaled = (w * np.exp2(127.0 - byte)[:, None, :]).reshape(k, n).astype(np.float32)
    by_word = np.ascontiguousarray(scaled.reshape(k // 512, 128, 4, n).transpose(0, 1, 3, 2))
    if fmt in ("e4m3", "e5m2"):
        words = by_word.astype(ml_dtypes.float8_e4m3fn if fmt == "e4m3" else ml_dtypes.float8_e5m2).view(np.uint8)
    else:
        c = by_word.astype(ml_dtypes.float4_e2m1fn).view(np.uint8) & 0xF
        words = (c[..., 0::2] | (c[..., 1::2] << 4)).reshape(k // 512, 128, 2 * n)
    return np.ascontiguousarray(words), np.ascontiguousarray(byte.astype(np.uint8).reshape(k // 512, 16, n))


def unpack_weight(words, scales, fmt):
    g, _, n = scales.shape
    words = np.ascontiguousarray(words).reshape(g, 128, n, -1)
    if fmt in ("e4m3", "e5m2"):
        vals = words.view(ml_dtypes.float8_e4m3fn if fmt == "e4m3" else ml_dtypes.float8_e5m2).astype(np.float64)
    else:
        nib = np.empty((g, 128, n, 4), np.uint8)
        nib[..., 0::2] = words & 0xF
        nib[..., 1::2] = words >> 4
        vals = E2M1[nib]
    vals = vals * np.repeat(np.exp2(scales.astype(np.float64) - 127.0), 8, axis=1)[..., None]
    return vals.transpose(0, 1, 3, 2).reshape(g * 512, n)


K, T, J, R, V, N = 1024, 1024, 384, 512, 512, 256


def setup_inputs():
    n = np.random.standard_normal
    idx = np.random.permutation(T)[:J]
    idx2 = np.random.permutation(V)[:J]
    fk = mx_kscale(K)
    fr = mx_kscale(R)
    wp = pack_weight(n((K, R)) * 1 / np.sqrt(K) * fk[:, None] * fr, "e5m2")
    wbp = pack_weight(n((R, N)) * 1 / np.sqrt(R) / fr[:, None], "e2m1")
    return {
        "xf": (n((K, T))).astype(np.float32),
        "fk": (np.random.uniform(0.5, 2.0, (K, 1)) / fk[:, None]).astype(np.float32),
        "w_words": wp[0],
        "w_scales": wp[1],
        "tb": (n((R, V)) * 0.7).astype(np.float32),
        "wb_words": wbp[0],
        "wb_scales": wbp[1],
        "rs": (1.0 * n((J, N))).astype(np.float32),
        "offs": striped(idx),
        "offs2": striped(idx2),
    }


def reference(xf, fk, w_words, w_scales, tb, wb_words, wb_scales, rs, offs, offs2):
    idx = unstriped(offs)
    idx2 = unstriped(offs2)
    wu = unpack_weight(w_words, w_scales, "e5m2")
    wbu = unpack_weight(wb_words, wb_scales, "e2m1")
    xg = f64(xf)[:, idx]
    x1 = np.pad(xg, ((0, 0), (1, 0)))[:, :J]
    u = (xg - 0.6 * x1) * f64(fk)
    uq = mxq(u, 0, "e4m3")
    a = wu.T @ uq
    hid = np.maximum(a, 0.0) * f64(tb)[:, idx2]
    hidq = mxq(hid, 0, "e4m3")
    p = hidq.T @ wbu
    pk2 = np.max(np.abs(p), axis=1, keepdims=True)
    y = p / (pk2 + 0.2) + 0.3 * f64(rs)
    return y

@@ -1,0 +1,266 @@
+from contextlib import ExitStack
+
+import concourse.mybir as mybir
+
+K, T, J, R, V, N = 1024, 1024, 384, 512, 512, 256
+FLOPS = 2 * K * R * J + 2 * R * J * N
+
+F32 = mybir.dt.float32
+BF16 = mybir.dt.bfloat16
+I32 = mybir.dt.int32
+U32 = mybir.dt.uint32
+U16 = mybir.dt.uint16
+U8 = mybir.dt.uint8
+E4M3 = mybir.dt.float8_e4m3fn_x4
+E5M2 = mybir.dt.float8_e5m2_x4
+E2M1 = mybir.dt.float4_e2m1fn_x4
+ALU = mybir.AluOpType
+ACT = mybir.ActivationFunctionType
+
+P = 128
+PACK = 4
+PASSES = K // (P * PACK)
+JT = J // P
+LEAD = 8
+ROW = LEAD + J
+COLS = P // 16
+
+
+def tile_list_steps_timestable_rowpeaks_kernel(
+    tc, xf, fk, w_words, w_scales, tb, wb_words, wb_scales, rs, offs, offs2, out
+):
+    nc = tc.nc
+    with ExitStack() as ctx:
+        lists = ctx.enter_context(tc.tile_pool(name="lists", bufs=1))
+        sb = ctx.enter_context(tc.tile_pool(name="sb", bufs=1))
+        ps = ctx.enter_context(tc.psum_pool(name="ps", bufs=1))
+
+        idx = lists.tile([P, J // 16], U16, name="idx")
+        idx2 = lists.tile([P, J // 16], U16, name="idx2")
+        x = [sb.tile([P, T], F32, name=f"x{q}") for q in range(PASSES * PACK)]
+        tbl = [sb.tile([P, V], F32, name=f"tbl{t}") for t in range(PACK)]
+        fks = sb.tile([P, PASSES * PACK], F32, name="fks")
+        zero = sb.tile([P, PASSES * PACK], F32, name="zero")
+        g = sb.tile([P, PASSES * PACK * ROW], F32, name="g")
+        d = [sb.tile([P, PACK * J], F32, name=f"d{z}") for z in range(PASSES)]
+        ub = [sb.tile([P, PACK * J], BF16, name=f"ub{z}", align_bytes=64) for z in range(PASSES)]
+        uq = [sb.tile([P, J], U32, name=f"uq{z}", align_bytes=64) for z in range(PASSES)]
+        us = [sb.tile([P, J], U8, name=f"us{z}", align_bytes=64) for z in range(PASSES)]
+        w_raw = [sb.tile([P, R], U32, name=f"w_raw{z}") for z in range(PASSES)]
+        wq = [sb.tile([P, R], U32, name=f"wq{z}", align_bytes=64) for z in range(PASSES)]
+        ws_raw = sb.tile([P, PASSES * R], U8, name="ws_raw")
+        ws = sb.tile([P, PASSES * R], U8, name="ws", align_bytes=64)
+        wbq = sb.tile([P, 2 * N], U8, name="wbq", align_bytes=64)
+        wbs = sb.tile([P, N], U8, name="wbs", align_bytes=64)
+        tg = [sb.tile([P, PACK * P], F32, name=f"tg{jt}") for jt in range(JT)]
+        rs_raw = sb.tile([P, JT * N], F32, name="rs_raw")
+        a = [ps.tile([P, PACK * P], F32, name=f"a{jt}") for jt in range(JT)]
+        pp = [ps.tile([P, N], F32, name=f"pp{jt}") for jt in range(JT)]
+
+        x_rows = xf.rearrange("(z p t) c -> z t p c", p=P, t=PACK)
+        tb_rows = tb.rearrange("(p t) c -> t p c", t=PACK)
+
+        def load_x(q):
+            nc.sync.dma_start(x[q][:], x_rows[q // PACK, q % PACK])
+
+        def load_tb(t):
+            nc.sync.dma_start(tbl[t][:], tb_rows[t])
+
+        def load_w(z):
+            nc.sync.dma_start(w_raw[z][:].bitcast(I32), w_words[z].rearrange("p c r -> p (c r)").bitcast(I32))
+
+        def load_ws(quad):
+            nc.sync.dma_start(
+                ws_raw[32 * quad : 32 * quad + 4, :].bitcast(I32).rearrange("p (z c) -> p z c", z=PASSES),
+                w_scales[:, 4 * quad : 4 * quad + 4, :].bitcast(I32).rearrange("z r c -> r z c"),
+            )
+
+        def load_wbs(quad):
+            nc.sync.dma_start(
+                wbs[32 * quad : 32 * quad + 4, :].bitcast(I32),
+                wb_scales[0, 4 * quad : 4 * quad + 4, :].bitcast(I32),
+            )
+
+        def gather_x(q, j0, j1):
+            base = q * ROW + LEAD
+            nc.scalar.activation(g[:, base + j0 : base + j1], x[q][:].indirect(idx[:, j0 // 16 : j1 // 16]), ACT.Copy)
+
+        def gather_tb(t, jt):
+            nc.scalar.activation(tg[jt][:, t * P : (t + 1) * P], tbl[t][:].indirect(idx2[:, jt * COLS : (jt + 1) * COLS]), ACT.Copy)
+
+        def step(q, j0, j1):
+            base = q * ROW + LEAD
+            t = q % PACK
+            nc.vector.scalar_tensor_tensor(
+                d[q // PACK][:, t * J + j0 : t * J + j1],
+                g[:, base + j0 - 1 : base + j1 - 1],
+                -0.6,
+                g[:, base + j0 : base + j1],
+                ALU.mult,
+                ALU.add,
+            )
+
+        def scale_pass(z):
+            nc.vector.tensor_tensor(
+                ub[z][:].rearrange("p (c i t) -> p c t i", i=2, t=PACK),
+                d[z][:].rearrange("p (t c i) -> p c t i", i=2, t=PACK),
+                fks[:, z * PACK : (z + 1) * PACK].rearrange("p (c t i) -> p c t i", c=1, i=1).to_broadcast([P, J // 2, PACK, 2]),
+                ALU.mult,
+            )
+
+        def scale_plane(q, j0, j1):
+            z, t = divmod(q, PACK)
+            nc.vector.tensor_scalar(
+                ub[z][:, PACK * j0 + t : PACK * j1 : PACK],
+                d[z][:, t * J + j0 : t * J + j1],
+                fks[:, q : q + 1],
+                None,
+                ALU.mult,
+            )
+
+        def quantize_u(z, j0, j1):
+            nc.vector.quantize_mx(uq[z][:, j0:j1].bitcast(E4M3), us[z][:, j0:j1], ub[z][:, PACK * j0 : PACK * j1])
+
+        def first_product(z, jt):
+            for t in range(PACK):
+                nc.tensor.matmul_mx(
+                    a[jt][:, t * P : (t + 1) * P],
+                    lhsT=wq[z][:, t * P : (t + 1) * P].bitcast(E5M2),
+                    lhsT_scale=ws[:, z * R + t * P : z * R + (t + 1) * P],
+                    rhs=uq[z][:, jt * P : (jt + 1) * P].bitcast(E4M3),
+                    rhs_scale=us[z][:, jt * P : (jt + 1) * P],
+                    start=(z == 0 and t == 0),
+                    stop=(z == PASSES - 1 and t == PACK - 1),
+                )
+
+        nc.vector.memset(ws_raw[:].bitcast(U32), 0)
+        nc.gpsimd.memset(zero[:], 0.0)
+        nc.gpsimd.memset(wbs[:].bitcast(U32), 0)
+        nc.scalar.activation(g[:, LEAD - 1 :: ROW], zero[:], ACT.Copy)
+
+        nc.sync.dma_start(idx[:], offs)
+        load_x(0)
+        for quad in range(4):
+            load_ws(quad)
+        load_x(1)
+        nc.sync.dma_start(
+            fks[:].rearrange("p (z t) -> p z t", z=PASSES), fk.rearrange("(z p t) o -> p z (t o)", p=P, t=PACK)
+        )
+        load_x(2)
+        nc.sync.dma_start(idx2[:], offs2)
+        load_x(3)
+        load_tb(0)
+        load_w(0)
+        load_x(4)
+        load_wbs(0)
+        load_x(5)
+        load_wbs(1)
+        load_x(6)
+        load_wbs(2)
+        load_x(7)
+        load_wbs(3)
+        load_w(1)
+        load_tb(1)
+        load_tb(2)
+        load_tb(3)
+        nc.sync.dma_start(wbq[:], wb_words[0])
+        nc.sync.dma_start(rs_raw[:].rearrange("p (j n) -> p j n", j=JT), rs.rearrange("(j p) n -> p j n", p=P))
+
+        nc.vector.tensor_copy(
+            ws[:].rearrange("p (z t m) -> p z m t", z=PASSES, t=PACK),
+            ws_raw[:].rearrange("p (z m t) -> p z m t", z=PASSES, t=PACK),
+        )
+        for q in range(PACK):
+            gather_x(q, 0, J)
+            step(q, 0, J)
+        scale_pass(0)
+        quantize_u(0, 0, J)
+        for jt in range(JT):
+            gather_tb(0, jt)
+        nc.scalar.copy(wq[0][:].rearrange("p (t m) -> p m t", t=PACK), w_raw[0][:].rearrange("p (m t) -> p m t", t=PACK))
+        for jt in range(JT):
+            first_product(0, jt)
+        for q in range(PACK, 2 * PACK - 1):
+            gather_x(q, 0, J)
+            step(q, 0, J)
+            scale_plane(q, 0, J)
+        last = 2 * PACK - 1
+        for jt in range(JT):
+            gather_x(last, jt * P, (jt + 1) * P)
+        step(last, 0, P)
+        step(last, P, 2 * P)
+        scale_plane(last, 0, P)
+        nc.vector.tensor_copy(wq[1][:].rearrange("p (t m) -> p m t", t=PACK), w_raw[1][:].rearrange("p (m t) -> p m t", t=PACK))
+        quantize_u(1, 0, P)
+        scale_plane(last, P, 2 * P)
+        step(last, 2 * P, 3 * P)
+        quantize_u(1, P, 2 * P)
+        scale_plane(last, 2 * P, 3 * P)
+        quantize_u(1, 2 * P, 3 * P)
+        for jt in range(JT):
+            first_product(1, jt)
+        for jt in range(JT):
+            gather_tb(1, jt)
+        for jt in range(JT):
+            gather_tb(2, jt)
+            gather_tb(3, jt)
+
+        hb = [sb.tile([P, PACK * P], BF16, name=f"hb{jt}", align_bytes=64) for jt in range(JT)]
+        hq = [sb.tile([P, P], U32, name=f"hq{jt}", align_bytes=64) for jt in range(JT)]
+        hs = [sb.tile([P, P], U8, name=f"hs{jt}", align_bytes=64) for jt in range(JT)]
+        res = [sb.tile([P, N], F32, name=f"res{jt}") for jt in range(JT)]
+        mag = [sb.tile([P, N], F32, name=f"mag{jt}") for jt in range(JT)]
+        den = [sb.tile([P, 1], F32, name=f"den{jt}") for jt in range(JT)]
+        inv = [sb.tile([P, 1], F32, name=f"inv{jt}") for jt in range(JT)]
+        y = [sb.tile([P, N], F32, name=f"y{jt}") for jt in range(JT)]
+
+        def hidden(jt):
+            nc.vector.scalar_tensor_tensor(
+                hb[jt][:].rearrange("p (j t) -> p j t", t=PACK),
+                a[jt][:].rearrange("p (t j) -> p j t", t=PACK),
+                0.0,
+                tg[jt][:].rearrange("p (t j) -> p j t", t=PACK),
+                ALU.max,
+                ALU.mult,
+            )
+
+        def second_product(jt):
+            nc.vector.quantize_mx(hq[jt][:].bitcast(E4M3), hs[jt][:], hb[jt][:])
+            nc.tensor.matmul_mx(
+                pp[jt][:],
+                lhsT=hq[jt][:].bitcast(E4M3),
+                lhsT_scale=hs[jt][:],
+                rhs=wbq[:].bitcast(E2M1),
+                rhs_scale=wbs[:],
+                start=True,
+                stop=True,
+            )
+            nc.scalar.activation(mag[jt][:], pp[jt][:], ACT.Abs)
+
+        def peak(jt):
+            nc.vector.tensor_scalar(mag[jt][:], mag[jt][:], 0.2, None, ALU.add, ALU.max, accum_out=den[jt][:])
+
+        def invert(jt):
+            nc.vector.reciprocal(inv[jt][:], den[jt][:])
+
+        def finish(jt):
+            nc.vector.scalar_tensor_tensor(y[jt][:], pp[jt][:], inv[jt][:], res[jt][:], ALU.mult, ALU.add)
+            nc.sync.dma_start(out[jt * P : (jt + 1) * P, :], y[jt][:])
+
+        for jt in range(JT):
+            nc.scalar.activation(res[jt][:], rs_raw[:, jt * N : (jt + 1) * N], ACT.Copy, scale=0.3)
+        hidden(0)
+        hidden(1)
+        second_product(0)
+        hidden(2)
+        second_product(1)
+        peak(0)
+        second_product(2)
+        invert(0)
+        peak(1)
+        finish(0)
+        invert(1)
+        peak(2)
+        finish(1)
+        invert(2)
+        finish(2)

@@ -24,6 +24,7 @@ JT = J // P
 LEAD = 8
 ROW = LEAD + J
 COLS = P // 16
+PARTS = ((0, P), (P, J))
 
 
 def tile_list_steps_timestable_rowpeaks_kernel(
@@ -43,16 +44,19 @@ def tile_list_steps_timestable_rowpeaks_kernel(
         zero = sb.tile([P, PASSES * PACK], F32, name="zero")
         g = sb.tile([P, PASSES * PACK * ROW], F32, name="g")
         d = [sb.tile([P, PACK * J], F32, name=f"d{z}") for z in range(PASSES)]
-        ub = [sb.tile([P, PACK * J], BF16, name=f"ub{z}", align_bytes=64) for z in range(PASSES)]
-        uq = [sb.tile([P, J], U32, name=f"uq{z}", align_bytes=64) for z in range(PASSES)]
-        us = [sb.tile([P, J], U8, name=f"us{z}", align_bytes=64) for z in range(PASSES)]
+        ub0 = sb.tile([P, PACK * J], BF16, name="ub0", align_bytes=64)
+        uq0 = sb.tile([P, J], U32, name="uq0", align_bytes=64)
+        us0 = sb.tile([P, J], U8, name="us0", align_bytes=64)
+        ub1 = [sb.tile([P, PACK * (j1 - j0)], BF16, name=f"ub1_{j0}", align_bytes=64) for j0, j1 in PARTS]
+        uq1 = [sb.tile([P, j1 - j0], U32, name=f"uq1_{j0}", align_bytes=64) for j0, j1 in PARTS]
+        us1 = [sb.tile([P, j1 - j0], U8, name=f"us1_{j0}", align_bytes=64) for j0, j1 in PARTS]
         w_raw = [sb.tile([P, R], U32, name=f"w_raw{z}") for z in range(PASSES)]
         wq = [sb.tile([P, R], U32, name=f"wq{z}", align_bytes=64) for z in range(PASSES)]
         ws_raw = sb.tile([P, PASSES * R], U8, name="ws_raw")
         ws = sb.tile([P, PASSES * R], U8, name="ws", align_bytes=64)
         wbq = sb.tile([P, 2 * N], U8, name="wbq", align_bytes=64)
         wbs = sb.tile([P, N], U8, name="wbs", align_bytes=64)
-        tg = [sb.tile([P, PACK * P], F32, name=f"tg{jt}") for jt in range(JT)]
+        tg = sb.tile([P, PACK * J], F32, name="tg")
         rs_raw = sb.tile([P, JT * N], F32, name="rs_raw")
         a = [ps.tile([P, PACK * P], F32, name=f"a{jt}") for jt in range(JT)]
         pp = [ps.tile([P, N], F32, name=f"pp{jt}") for jt in range(JT)]
@@ -85,8 +89,8 @@ def tile_list_steps_timestable_rowpeaks_kernel(
             base = q * ROW + LEAD
             nc.scalar.activation(g[:, base + j0 : base + j1], x[q][:].indirect(idx[:, j0 // 16 : j1 // 16]), ACT.Copy)
 
-        def gather_tb(t, jt):
-            nc.scalar.activation(tg[jt][:, t * P : (t + 1) * P], tbl[t][:].indirect(idx2[:, jt * COLS : (jt + 1) * COLS]), ACT.Copy)
+        def gather_tb(t, j0, j1):
+            nc.scalar.activation(tg[:, t * J + j0 : t * J + j1], tbl[t][:].indirect(idx2[:, j0 // 16 : j1 // 16]), ACT.Copy)
 
         def step(q, j0, j1):
             base = q * ROW + LEAD
@@ -100,40 +104,36 @@ def tile_list_steps_timestable_rowpeaks_kernel(
                 ALU.add,
             )
 
-        def scale_pass(z):
+        def scale(dst, z, j0, j1):
             nc.vector.tensor_tensor(
-                ub[z][:].rearrange("p (c i t) -> p c t i", i=2, t=PACK),
-                d[z][:].rearrange("p (t c i) -> p c t i", i=2, t=PACK),
-                fks[:, z * PACK : (z + 1) * PACK].rearrange("p (c t i) -> p c t i", c=1, i=1).to_broadcast([P, J // 2, PACK, 2]),
+                dst.rearrange("p (c i t) -> p c t i", i=2, t=PACK),
+                d[z][:].rearrange("p (t c i) -> p c t i", i=2, t=PACK)[:, j0 // 2 : j1 // 2],
+                fks[:, z * PACK : (z + 1) * PACK]
+                .rearrange("p (c t i) -> p c t i", c=1, i=1)
+                .to_broadcast([P, (j1 - j0) // 2, PACK, 2]),
                 ALU.mult,
             )
 
-        def scale_plane(q, j0, j1):
-            z, t = divmod(q, PACK)
-            nc.vector.tensor_scalar(
-                ub[z][:, PACK * j0 + t : PACK * j1 : PACK],
-                d[z][:, t * J + j0 : t * J + j1],
-                fks[:, q : q + 1],
-                None,
-                ALU.mult,
-            )
-
-        def quantize_u(z, j0, j1):
-            nc.vector.quantize_mx(uq[z][:, j0:j1].bitcast(E4M3), us[z][:, j0:j1], ub[z][:, PACK * j0 : PACK * j1])
+        def order_w(copy, z):
+            copy(wq[z][:].rearrange("p (t m) -> p m t", t=PACK), w_raw[z][:].rearrange("p (m t) -> p m t", t=PACK))
 
         def first_product(z, jt):
+            part = min(jt, 1)
+            at = slice((jt - part) * P, (jt - part + 1) * P)
+            codes = uq0[:, jt * P : (jt + 1) * P] if z == 0 else uq1[part][:, at]
+            scales = us0[:, jt * P : (jt + 1) * P] if z == 0 else us1[part][:, at]
             for t in range(PACK):
                 nc.tensor.matmul_mx(
                     a[jt][:, t * P : (t + 1) * P],
                     lhsT=wq[z][:, t * P : (t + 1) * P].bitcast(E5M2),
                     lhsT_scale=ws[:, z * R + t * P : z * R + (t + 1) * P],
-                    rhs=uq[z][:, jt * P : (jt + 1) * P].bitcast(E4M3),
-                    rhs_scale=us[z][:, jt * P : (jt + 1) * P],
+                    rhs=codes.bitcast(E4M3),
+                    rhs_scale=scales,
                     start=(z == 0 and t == 0),
                     stop=(z == PASSES - 1 and t == PACK - 1),
                 )
 
-        nc.vector.memset(ws_raw[:].bitcast(U32), 0)
+        nc.gpsimd.memset(ws_raw[:].bitcast(U32), 0)
         nc.gpsimd.memset(zero[:], 0.0)
         nc.gpsimd.memset(wbs[:].bitcast(U32), 0)
         nc.scalar.activation(g[:, LEAD - 1 :: ROW], zero[:], ACT.Copy)
@@ -149,20 +149,13 @@ def tile_list_steps_timestable_rowpeaks_kernel(
         load_x(2)
         nc.sync.dma_start(idx2[:], offs2)
         load_x(3)
-        load_tb(0)
         load_w(0)
-        load_x(4)
-        load_wbs(0)
-        load_x(5)
-        load_wbs(1)
-        load_x(6)
-        load_wbs(2)
-        load_x(7)
-        load_wbs(3)
+        for q in range(PACK, 2 * PACK):
+            load_x(q)
+            load_wbs(q - PACK)
         load_w(1)
-        load_tb(1)
-        load_tb(2)
-        load_tb(3)
+        for t in range(PACK):
+            load_tb(t)
         nc.sync.dma_start(wbq[:], wb_words[0])
         nc.sync.dma_start(rs_raw[:].rearrange("p (j n) -> p j n", j=JT), rs.rearrange("(j p) n -> p j n", p=P))
 
@@ -173,37 +166,24 @@ def tile_list_steps_timestable_rowpeaks_kernel(
         for q in range(PACK):
             gather_x(q, 0, J)
             step(q, 0, J)
-        scale_pass(0)
-        quantize_u(0, 0, J)
-        for jt in range(JT):
-            gather_tb(0, jt)
-        nc.scalar.copy(wq[0][:].rearrange("p (t m) -> p m t", t=PACK), w_raw[0][:].rearrange("p (m t) -> p m t", t=PACK))
+        scale(ub0[:], 0, 0, J)
+        nc.vector.quantize_mx(uq0[:].bitcast(E4M3), us0[:], ub0[:])
+        order_w(nc.scalar.copy, 0)
         for jt in range(JT):
             first_product(0, jt)
-        for q in range(PACK, 2 * PACK - 1):
+        for q in range(PACK, 2 * PACK):
             gather_x(q, 0, J)
             step(q, 0, J)
-            scale_plane(q, 0, J)
-        last = 2 * PACK - 1
-        for jt in range(JT):
-            gather_x(last, jt * P, (jt + 1) * P)
-        step(last, 0, P)
-        step(last, P, 2 * P)
-        scale_plane(last, 0, P)
-        nc.vector.tensor_copy(wq[1][:].rearrange("p (t m) -> p m t", t=PACK), w_raw[1][:].rearrange("p (m t) -> p m t", t=PACK))
-        quantize_u(1, 0, P)
-        scale_plane(last, P, 2 * P)
-        step(last, 2 * P, 3 * P)
-        quantize_u(1, P, 2 * P)
-        scale_plane(last, 2 * P, 3 * P)
-        quantize_u(1, 2 * P, 3 * P)
+        order_w(nc.vector.tensor_copy, 1)
+        for part, (j0, j1) in enumerate(PARTS):
+            scale(ub1[part][:], 1, j0, j1)
+            nc.vector.quantize_mx(uq1[part][:].bitcast(E4M3), us1[part][:], ub1[part][:])
         for jt in range(JT):
             first_product(1, jt)
+        for t in range(PACK - 1):
+            gather_tb(t, 0, J)
         for jt in range(JT):
-            gather_tb(1, jt)
-        for jt in range(JT):
-            gather_tb(2, jt)
-            gather_tb(3, jt)
+            gather_tb(PACK - 1, jt * P, (jt + 1) * P)
 
         hb = [sb.tile([P, PACK * P], BF16, name=f"hb{jt}", align_bytes=64) for jt in range(JT)]
         hq = [sb.tile([P, P], U32, name=f"hq{jt}", align_bytes=64) for jt in range(JT)]
@@ -212,6 +192,7 @@ def tile_list_steps_timestable_rowpeaks_kernel(
         mag = [sb.tile([P, N], F32, name=f"mag{jt}") for jt in range(JT)]
         den = [sb.tile([P, 1], F32, name=f"den{jt}") for jt in range(JT)]
         inv = [sb.tile([P, 1], F32, name=f"inv{jt}") for jt in range(JT)]
+        scaled = sb.tile([P, N], F32, name="scaled")
         y = [sb.tile([P, N], F32, name=f"y{jt}") for jt in range(JT)]
 
         def hidden(jt):
@@ -219,7 +200,7 @@ def tile_list_steps_timestable_rowpeaks_kernel(
                 hb[jt][:].rearrange("p (j t) -> p j t", t=PACK),
                 a[jt][:].rearrange("p (t j) -> p j t", t=PACK),
                 0.0,
-                tg[jt][:].rearrange("p (t j) -> p j t", t=PACK),
+                tg[:].rearrange("p (t j) -> p j t", t=PACK)[:, jt * P : (jt + 1) * P, :],
                 ALU.max,
                 ALU.mult,
             )
@@ -244,7 +225,11 @@ def tile_list_steps_timestable_rowpeaks_kernel(
             nc.vector.reciprocal(inv[jt][:], den[jt][:])
 
         def finish(jt):
-            nc.vector.scalar_tensor_tensor(y[jt][:], pp[jt][:], inv[jt][:], res[jt][:], ALU.mult, ALU.add)
+            if jt > 0:
+                nc.vector.scalar_tensor_tensor(y[jt][:], pp[jt][:], inv[jt][:], res[jt][:], ALU.mult, ALU.add)
+            else:
+                nc.scalar.activation(scaled[:], pp[jt][:], ACT.Copy, scale=inv[jt][:])
+                nc.gpsimd.tensor_tensor(y[jt][:], scaled[:], res[jt][:], ALU.add)
             nc.sync.dma_start(out[jt * P : (jt + 1) * P, :], y[jt][:])
 
         for jt in range(JT):

@@ -20,11 +20,14 @@ ACT = mybir.ActivationFunctionType
 P = 128
 PACK = 4
 PASSES = K // (P * PACK)
-JT = J // P
+PLANES = PASSES * PACK
+TILES = J // P
+QUADS = 4
+SCALE_ROWS = 4
+PER_COLUMN = 16
 LEAD = 8
 ROW = LEAD + J
-COLS = P // 16
-PARTS = ((0, P), (P, J))
+PAIR = 2
 
 
 def tile_list_steps_timestable_rowpeaks_kernel(
@@ -36,30 +39,32 @@ def tile_list_steps_timestable_rowpeaks_kernel(
         sb = ctx.enter_context(tc.tile_pool(name="sb", bufs=1))
         ps = ctx.enter_context(tc.psum_pool(name="ps", bufs=1))
 
-        idx = lists.tile([P, J // 16], U16, name="idx")
-        idx2 = lists.tile([P, J // 16], U16, name="idx2")
-        x = [sb.tile([P, T], F32, name=f"x{q}") for q in range(PASSES * PACK)]
-        tbl = [sb.tile([P, V], F32, name=f"tbl{t}") for t in range(PACK)]
-        fks = sb.tile([P, PASSES * PACK], F32, name="fks")
-        zero = sb.tile([P, PASSES * PACK], F32, name="zero")
-        g = sb.tile([P, PASSES * PACK * ROW], F32, name="g")
-        d = [sb.tile([P, PACK * J], F32, name=f"d{z}") for z in range(PASSES)]
-        ub0 = sb.tile([P, PACK * J], BF16, name="ub0", align_bytes=64)
-        uq0 = sb.tile([P, J], U32, name="uq0", align_bytes=64)
-        us0 = sb.tile([P, J], U8, name="us0", align_bytes=64)
-        ub1 = [sb.tile([P, PACK * (j1 - j0)], BF16, name=f"ub1_{j0}", align_bytes=64) for j0, j1 in PARTS]
-        uq1 = [sb.tile([P, j1 - j0], U32, name=f"uq1_{j0}", align_bytes=64) for j0, j1 in PARTS]
-        us1 = [sb.tile([P, j1 - j0], U8, name=f"us1_{j0}", align_bytes=64) for j0, j1 in PARTS]
+        idx = lists.tile([P, J // PER_COLUMN], U16, name="idx")
+        idx2 = lists.tile([P, J // PER_COLUMN], U16, name="idx2")
+        x = [sb.tile([P, T], F32, name=f"x{q}") for q in range(PLANES)]
+        tb_early = [sb.tile([P, V], F32, name=f"tb{t}") for t in range(PACK // 2)]
+        tb_late = sb.tile([P, 2 * V], F32, name="tb_late")
+        tb_plane = [tb_early[0][:], tb_early[1][:], tb_late[:, :V], tb_late[:, V:]]
+        factor = sb.tile([P, PLANES], F32, name="factor")
+        zero = sb.tile([P, PLANES], F32, name="zero")
+        xg = sb.tile([P, PLANES * ROW], F32, name="xg")
+        steps = [sb.tile([P, PACK * J], F32, name=f"steps{z}") for z in range(PASSES)]
+        u0 = sb.tile([P, PACK * J], BF16, name="u0", align_bytes=64)
+        u0_codes = sb.tile([P, J], U32, name="u0_codes", align_bytes=64)
+        u0_scales = sb.tile([P, J], U8, name="u0_scales", align_bytes=64)
+        u1 = [sb.tile([P, PACK * P], BF16, name=f"u1_{jt}", align_bytes=64) for jt in range(TILES)]
+        u1_codes = [sb.tile([P, P], U32, name=f"u1_codes{jt}", align_bytes=64) for jt in range(TILES)]
+        u1_scales = [sb.tile([P, P], U8, name=f"u1_scales{jt}", align_bytes=64) for jt in range(TILES)]
         w_raw = [sb.tile([P, R], U32, name=f"w_raw{z}") for z in range(PASSES)]
-        wq = [sb.tile([P, R], U32, name=f"wq{z}", align_bytes=64) for z in range(PASSES)]
+        w_codes = [sb.tile([P, R], U32, name=f"w_codes{z}", align_bytes=64) for z in range(PASSES)]
         ws_raw = sb.tile([P, PASSES * R], U8, name="ws_raw")
         ws = sb.tile([P, PASSES * R], U8, name="ws", align_bytes=64)
-        wbq = sb.tile([P, 2 * N], U8, name="wbq", align_bytes=64)
+        wb_codes = sb.tile([P, 2 * N], U8, name="wb_codes", align_bytes=64)
         wbs = sb.tile([P, N], U8, name="wbs", align_bytes=64)
         tg = sb.tile([P, PACK * J], F32, name="tg")
-        rs_raw = sb.tile([P, JT * N], F32, name="rs_raw")
-        a = [ps.tile([P, PACK * P], F32, name=f"a{jt}") for jt in range(JT)]
-        pp = [ps.tile([P, N], F32, name=f"pp{jt}") for jt in range(JT)]
+        rs_raw = sb.tile([P, TILES * N], F32, name="rs_raw")
+        a = [ps.tile([P, PACK * P], F32, name=f"a{jt}") for jt in range(TILES)]
+        prod = [ps.tile([P, N], F32, name=f"prod{jt}") for jt in range(TILES)]
 
         x_rows = xf.rearrange("(z p t) c -> z t p c", p=P, t=PACK)
         tb_rows = tb.rearrange("(p t) c -> t p c", t=PACK)
@@ -67,65 +72,50 @@ def tile_list_steps_timestable_rowpeaks_kernel(
         def load_x(q):
             nc.sync.dma_start(x[q][:], x_rows[q // PACK, q % PACK])
 
-        def load_tb(t):
-            nc.sync.dma_start(tbl[t][:], tb_rows[t])
+        def scale_rows(plane, quad):
+            return plane[32 * quad : 32 * quad + SCALE_ROWS, :].bitcast(I32)
 
-        def load_w(z):
-            nc.sync.dma_start(w_raw[z][:].bitcast(I32), w_words[z].rearrange("p c r -> p (c r)").bitcast(I32))
-
-        def load_ws(quad):
-            nc.sync.dma_start(
-                ws_raw[32 * quad : 32 * quad + 4, :].bitcast(I32).rearrange("p (z c) -> p z c", z=PASSES),
-                w_scales[:, 4 * quad : 4 * quad + 4, :].bitcast(I32).rearrange("z r c -> r z c"),
-            )
-
-        def load_wbs(quad):
-            nc.sync.dma_start(
-                wbs[32 * quad : 32 * quad + 4, :].bitcast(I32),
-                wb_scales[0, 4 * quad : 4 * quad + 4, :].bitcast(I32),
-            )
-
-        def gather_x(q, j0, j1):
-            base = q * ROW + LEAD
-            nc.scalar.activation(g[:, base + j0 : base + j1], x[q][:].indirect(idx[:, j0 // 16 : j1 // 16]), ACT.Copy)
+        def gather_x(q):
+            first = q * ROW + LEAD
+            nc.scalar.activation(xg[:, first : first + J], x[q][:].indirect(idx[:]), ACT.Copy)
 
         def gather_tb(t, j0, j1):
-            nc.scalar.activation(tg[:, t * J + j0 : t * J + j1], tbl[t][:].indirect(idx2[:, j0 // 16 : j1 // 16]), ACT.Copy)
+            entries = idx2[:, j0 // PER_COLUMN : j1 // PER_COLUMN]
+            nc.scalar.activation(tg[:, t * J + j0 : t * J + j1], tb_plane[t].indirect(entries), ACT.Copy)
 
-        def step(q, j0, j1):
-            base = q * ROW + LEAD
-            t = q % PACK
+        def step(q):
+            z, t = divmod(q, PACK)
+            first = q * ROW + LEAD
             nc.vector.scalar_tensor_tensor(
-                d[q // PACK][:, t * J + j0 : t * J + j1],
-                g[:, base + j0 - 1 : base + j1 - 1],
+                steps[z][:, t * J : (t + 1) * J],
+                xg[:, first - 1 : first + J - 1],
                 -0.6,
-                g[:, base + j0 : base + j1],
+                xg[:, first : first + J],
                 ALU.mult,
                 ALU.add,
             )
 
         def scale(dst, z, j0, j1):
             nc.vector.tensor_tensor(
-                dst.rearrange("p (c i t) -> p c t i", i=2, t=PACK),
-                d[z][:].rearrange("p (t c i) -> p c t i", i=2, t=PACK)[:, j0 // 2 : j1 // 2],
-                fks[:, z * PACK : (z + 1) * PACK]
+                dst.rearrange("p (c i t) -> p c t i", i=PAIR, t=PACK),
+                steps[z][:].rearrange("p (t c i) -> p c t i", i=PAIR, t=PACK)[:, j0 // PAIR : j1 // PAIR],
+                factor[:, z * PACK : (z + 1) * PACK]
                 .rearrange("p (c t i) -> p c t i", c=1, i=1)
-                .to_broadcast([P, (j1 - j0) // 2, PACK, 2]),
+                .to_broadcast([P, (j1 - j0) // PAIR, PACK, PAIR]),
                 ALU.mult,
             )
 
         def order_w(copy, z):
-            copy(wq[z][:].rearrange("p (t m) -> p m t", t=PACK), w_raw[z][:].rearrange("p (m t) -> p m t", t=PACK))
+            copy(
+                w_codes[z][:].rearrange("p (t m) -> p m t", t=PACK),
+                w_raw[z][:].rearrange("p (m t) -> p m t", t=PACK),
+            )
 
-        def first_product(z, jt):
-            part = min(jt, 1)
-            at = slice((jt - part) * P, (jt - part + 1) * P)
-            codes = uq0[:, jt * P : (jt + 1) * P] if z == 0 else uq1[part][:, at]
-            scales = us0[:, jt * P : (jt + 1) * P] if z == 0 else us1[part][:, at]
+        def first_product(z, jt, codes, scales):
             for t in range(PACK):
                 nc.tensor.matmul_mx(
                     a[jt][:, t * P : (t + 1) * P],
-                    lhsT=wq[z][:, t * P : (t + 1) * P].bitcast(E5M2),
+                    lhsT=w_codes[z][:, t * P : (t + 1) * P].bitcast(E5M2),
                     lhsT_scale=ws[:, z * R + t * P : z * R + (t + 1) * P],
                     rhs=codes.bitcast(E4M3),
                     rhs_scale=scales,
@@ -136,68 +126,85 @@ def tile_list_steps_timestable_rowpeaks_kernel(
         nc.gpsimd.memset(ws_raw[:].bitcast(U32), 0)
         nc.gpsimd.memset(zero[:], 0.0)
         nc.gpsimd.memset(wbs[:].bitcast(U32), 0)
-        nc.scalar.activation(g[:, LEAD - 1 :: ROW], zero[:], ACT.Copy)
+        nc.scalar.activation(xg[:, LEAD - 1 :: ROW], zero[:], ACT.Copy)
 
         nc.sync.dma_start(idx[:], offs)
         load_x(0)
-        for quad in range(4):
-            load_ws(quad)
-        load_x(1)
-        nc.sync.dma_start(
-            fks[:].rearrange("p (z t) -> p z t", z=PASSES), fk.rearrange("(z p t) o -> p z (t o)", p=P, t=PACK)
-        )
-        load_x(2)
-        nc.sync.dma_start(idx2[:], offs2)
-        load_x(3)
-        load_w(0)
-        for q in range(PACK, 2 * PACK):
+        for quad in range(QUADS):
+            nc.sync.dma_start(
+                scale_rows(ws_raw, quad).rearrange("p (z c) -> p z c", z=PASSES),
+                w_scales[:, SCALE_ROWS * quad : SCALE_ROWS * (quad + 1), :].bitcast(I32).rearrange("z r c -> r z c"),
+            )
+        for q in range(1, PACK):
             load_x(q)
-            load_wbs(q - PACK)
-        load_w(1)
-        for t in range(PACK):
-            load_tb(t)
-        nc.sync.dma_start(wbq[:], wb_words[0])
-        nc.sync.dma_start(rs_raw[:].rearrange("p (j n) -> p j n", j=JT), rs.rearrange("(j p) n -> p j n", p=P))
+        nc.sync.dma_start(
+            factor[:].rearrange("p (z t) -> p z t", z=PASSES), fk.rearrange("(z p t) o -> p z (t o)", p=P, t=PACK)
+        )
+        nc.sync.dma_start(idx2[:], offs2)
+        for q in range(PACK, PLANES):
+            load_x(q)
+        for z in range(PASSES):
+            nc.sync.dma_start(w_raw[z][:].bitcast(I32), w_words[z].rearrange("p c r -> p (c r)").bitcast(I32))
+        for t in range(PACK // 2):
+            nc.sync.dma_start(tb_plane[t], tb_rows[t])
+        nc.sync.dma_start(tb_late[:], tb.rearrange("(p h t) c -> h p (t c)", h=2, t=2)[1])
+        nc.sync.dma_start(wb_codes[:], wb_words[0])
+        nc.sync.dma_start(rs_raw[:].rearrange("p (j n) -> p j n", j=TILES), rs.rearrange("(j p) n -> p j n", p=P))
+        for quad in range(QUADS):
+            nc.sync.dma_start(
+                scale_rows(wbs, quad), wb_scales[0, SCALE_ROWS * quad : SCALE_ROWS * (quad + 1), :].bitcast(I32)
+            )
 
         nc.vector.tensor_copy(
-            ws[:].rearrange("p (z t m) -> p z m t", z=PASSES, t=PACK),
-            ws_raw[:].rearrange("p (z m t) -> p z m t", z=PASSES, t=PACK),
+            ws[:].rearrange("p (z t m) -> p z t m", z=PASSES, t=PACK),
+            ws_raw[:].rearrange("p (z m t) -> p z t m", z=PASSES, t=PACK),
         )
-        for q in range(PACK):
-            gather_x(q, 0, J)
-            step(q, 0, J)
-        scale(ub0[:], 0, 0, J)
-        nc.vector.quantize_mx(uq0[:].bitcast(E4M3), us0[:], ub0[:])
-        order_w(nc.scalar.copy, 0)
-        for jt in range(JT):
-            first_product(0, jt)
-        for q in range(PACK, 2 * PACK):
-            gather_x(q, 0, J)
-            step(q, 0, J)
-        order_w(nc.vector.tensor_copy, 1)
-        for part, (j0, j1) in enumerate(PARTS):
-            scale(ub1[part][:], 1, j0, j1)
-            nc.vector.quantize_mx(uq1[part][:].bitcast(E4M3), us1[part][:], ub1[part][:])
-        for jt in range(JT):
-            first_product(1, jt)
-        for t in range(PACK - 1):
-            gather_tb(t, 0, J)
-        for jt in range(JT):
-            gather_tb(PACK - 1, jt * P, (jt + 1) * P)
 
-        hb = [sb.tile([P, PACK * P], BF16, name=f"hb{jt}", align_bytes=64) for jt in range(JT)]
-        hq = [sb.tile([P, P], U32, name=f"hq{jt}", align_bytes=64) for jt in range(JT)]
-        hs = [sb.tile([P, P], U8, name=f"hs{jt}", align_bytes=64) for jt in range(JT)]
-        res = [sb.tile([P, N], F32, name=f"res{jt}") for jt in range(JT)]
-        mag = [sb.tile([P, N], F32, name=f"mag{jt}") for jt in range(JT)]
-        den = [sb.tile([P, 1], F32, name=f"den{jt}") for jt in range(JT)]
-        inv = [sb.tile([P, 1], F32, name=f"inv{jt}") for jt in range(JT)]
-        scaled = sb.tile([P, N], F32, name="scaled")
-        y = [sb.tile([P, N], F32, name=f"y{jt}") for jt in range(JT)]
+        for q in range(PACK):
+            gather_x(q)
+            step(q)
+        scale(u0[:], 0, 0, J)
+        gather_x(PACK)
+        step(PACK)
+        nc.vector.quantize_mx(u0_codes[:].bitcast(E4M3), u0_scales[:], u0[:])
+        for q in range(PACK + 1, PLANES):
+            gather_x(q)
+            step(q)
+
+        order_w(nc.scalar.copy, 0)
+        order_w(nc.vector.tensor_copy, 1)
+        for jt in range(TILES):
+            slots = slice(jt * P, (jt + 1) * P)
+            first_product(0, jt, u0_codes[:, slots], u0_scales[:, slots])
+
+        def quantize_u1(jt):
+            nc.vector.quantize_mx(u1_codes[jt][:].bitcast(E4M3), u1_scales[jt][:], u1[jt][:])
+            first_product(1, jt, u1_codes[jt][:], u1_scales[jt][:])
+
+        scale(u1[0][:], 1, 0, P)
+        for jt in range(1, TILES):
+            scale(u1[jt][:], 1, jt * P, (jt + 1) * P)
+            quantize_u1(jt - 1)
+        quantize_u1(TILES - 1)
+
+        for t in range(PACK // 2):
+            gather_tb(t, 0, J)
+        for jt in range(TILES):
+            for t in range(PACK // 2, PACK):
+                gather_tb(t, jt * P, (jt + 1) * P)
+
+        hid = [sb.tile([P, PACK * P], BF16, name=f"hid{jt}", align_bytes=64) for jt in range(TILES)]
+        hid_codes = [sb.tile([P, P], U32, name=f"hid_codes{jt}", align_bytes=64) for jt in range(TILES)]
+        hid_scales = [sb.tile([P, P], U8, name=f"hid_scales{jt}", align_bytes=64) for jt in range(TILES)]
+        res = [sb.tile([P, N], F32, name=f"res{jt}") for jt in range(TILES)]
+        mag = [sb.tile([P, N], F32, name=f"mag{jt}") for jt in range(TILES)]
+        den = [sb.tile([P, 1], F32, name=f"den{jt}") for jt in range(TILES)]
+        inv = [sb.tile([P, 1], F32, name=f"inv{jt}") for jt in range(TILES)]
+        y = [sb.tile([P, N], F32, name=f"y{jt}") for jt in range(TILES)]
 
         def hidden(jt):
             nc.vector.scalar_tensor_tensor(
-                hb[jt][:].rearrange("p (j t) -> p j t", t=PACK),
+                hid[jt][:].rearrange("p (j t) -> p j t", t=PACK),
                 a[jt][:].rearrange("p (t j) -> p j t", t=PACK),
                 0.0,
                 tg[:].rearrange("p (t j) -> p j t", t=PACK)[:, jt * P : (jt + 1) * P, :],
@@ -206,17 +213,17 @@ def tile_list_steps_timestable_rowpeaks_kernel(
             )
 
         def second_product(jt):
-            nc.vector.quantize_mx(hq[jt][:].bitcast(E4M3), hs[jt][:], hb[jt][:])
+            nc.vector.quantize_mx(hid_codes[jt][:].bitcast(E4M3), hid_scales[jt][:], hid[jt][:])
             nc.tensor.matmul_mx(
-                pp[jt][:],
-                lhsT=hq[jt][:].bitcast(E4M3),
-                lhsT_scale=hs[jt][:],
-                rhs=wbq[:].bitcast(E2M1),
+                prod[jt][:],
+                lhsT=hid_codes[jt][:].bitcast(E4M3),
+                lhsT_scale=hid_scales[jt][:],
+                rhs=wb_codes[:].bitcast(E2M1),
                 rhs_scale=wbs[:],
                 start=True,
                 stop=True,
             )
-            nc.scalar.activation(mag[jt][:], pp[jt][:], ACT.Abs)
+            nc.scalar.activation(mag[jt][:], prod[jt][:], ACT.Abs)
 
         def peak(jt):
             nc.vector.tensor_scalar(mag[jt][:], mag[jt][:], 0.2, None, ALU.add, ALU.max, accum_out=den[jt][:])
@@ -225,15 +232,12 @@ def tile_list_steps_timestable_rowpeaks_kernel(
             nc.vector.reciprocal(inv[jt][:], den[jt][:])
 
         def finish(jt):
-            if jt > 0:
-                nc.vector.scalar_tensor_tensor(y[jt][:], pp[jt][:], inv[jt][:], res[jt][:], ALU.mult, ALU.add)
-            else:
-                nc.scalar.activation(scaled[:], pp[jt][:], ACT.Copy, scale=inv[jt][:])
-                nc.gpsimd.tensor_tensor(y[jt][:], scaled[:], res[jt][:], ALU.add)
+            nc.vector.scalar_tensor_tensor(y[jt][:], prod[jt][:], inv[jt][:], res[jt][:], ALU.mult, ALU.add)
             nc.sync.dma_start(out[jt * P : (jt + 1) * P, :], y[jt][:])
 
-        for jt in range(JT):
+        for jt in range(TILES):
             nc.scalar.activation(res[jt][:], rs_raw[:, jt * N : (jt + 1) * N], ACT.Copy, scale=0.3)
+
         hidden(0)
         hidden(1)
         second_product(0)

@@ -25,7 +25,8 @@ TILES = J // P
 QUADS = 4
 SCALE_ROWS = 4
 PER_COLUMN = 16
-LEAD = 8
+BLOCK = 8
+LEAD = BLOCK
 ROW = LEAD + J
 PAIR = 2
 
@@ -45,7 +46,7 @@ def tile_list_steps_timestable_rowpeaks_kernel(
         tb_early = [sb.tile([P, V], F32, name=f"tb{t}") for t in range(PACK // 2)]
         tb_late = sb.tile([P, 2 * V], F32, name="tb_late")
         tb_plane = [tb_early[0][:], tb_early[1][:], tb_late[:, :V], tb_late[:, V:]]
-        factor = sb.tile([P, PLANES], F32, name="factor")
+        factor = sb.tile([P, PASSES, BLOCK], F32, name="factor")
         zero = sb.tile([P, PLANES], F32, name="zero")
         xg = sb.tile([P, PLANES * ROW], F32, name="xg")
         steps = [sb.tile([P, PACK * J], F32, name=f"steps{z}") for z in range(PASSES)]
@@ -99,7 +100,7 @@ def tile_list_steps_timestable_rowpeaks_kernel(
             nc.vector.tensor_tensor(
                 dst.rearrange("p (c i t) -> p c t i", i=PAIR, t=PACK),
                 steps[z][:].rearrange("p (t c i) -> p c t i", i=PAIR, t=PACK)[:, j0 // PAIR : j1 // PAIR],
-                factor[:, z * PACK : (z + 1) * PACK]
+                factor[:, z, :PACK]
                 .rearrange("p (c t i) -> p c t i", c=1, i=1)
                 .to_broadcast([P, (j1 - j0) // PAIR, PACK, PAIR]),
                 ALU.mult,
@@ -137,9 +138,7 @@ def tile_list_steps_timestable_rowpeaks_kernel(
             )
         for q in range(1, PACK):
             load_x(q)
-        nc.sync.dma_start(
-            factor[:].rearrange("p (z t) -> p z t", z=PASSES), fk.rearrange("(z p t) o -> p z (t o)", p=P, t=PACK)
-        )
+        nc.sync.dma_start(factor[:, :, :PACK], fk.rearrange("(z p t) o -> p z (t o)", p=P, t=PACK))
         nc.sync.dma_start(idx2[:], offs2)
         for q in range(PACK, PLANES):
             load_x(q)
@@ -200,6 +199,7 @@ def tile_list_steps_timestable_rowpeaks_kernel(
         mag = [sb.tile([P, N], F32, name=f"mag{jt}") for jt in range(TILES)]
         den = [sb.tile([P, 1], F32, name=f"den{jt}") for jt in range(TILES)]
         inv = [sb.tile([P, 1], F32, name=f"inv{jt}") for jt in range(TILES)]
+        scaled = sb.tile([P, N], F32, name="scaled")
         y = [sb.tile([P, N], F32, name=f"y{jt}") for jt in range(TILES)]
 
         def hidden(jt):
@@ -235,6 +235,11 @@ def tile_list_steps_timestable_rowpeaks_kernel(
             nc.vector.scalar_tensor_tensor(y[jt][:], prod[jt][:], inv[jt][:], res[jt][:], ALU.mult, ALU.add)
             nc.sync.dma_start(out[jt * P : (jt + 1) * P, :], y[jt][:])
 
+        def finish_beside_vector(jt):
+            nc.scalar.activation(scaled[:], prod[jt][:], ACT.Copy, scale=inv[jt][:])
+            nc.gpsimd.tensor_tensor(y[jt][:], scaled[:], res[jt][:], ALU.add)
+            nc.sync.dma_start(out[jt * P : (jt + 1) * P, :], y[jt][:])
+
         for jt in range(TILES):
             nc.scalar.activation(res[jt][:], rs_raw[:, jt * N : (jt + 1) * N], ACT.Copy, scale=0.3)
 
@@ -247,7 +252,7 @@ def tile_list_steps_timestable_rowpeaks_kernel(
         second_product(2)
         invert(0)
         peak(1)
-        finish(0)
+        finish_beside_vector(0)
         invert(1)
         peak(2)
         finish(1)

from contextlib import ExitStack

import concourse.mybir as mybir

K, T, J, R, V, N = 1024, 1024, 384, 512, 512, 256
FLOPS = 2 * K * R * J + 2 * R * J * N

F32 = mybir.dt.float32
BF16 = mybir.dt.bfloat16
I32 = mybir.dt.int32
U32 = mybir.dt.uint32
U16 = mybir.dt.uint16
U8 = mybir.dt.uint8
E4M3 = mybir.dt.float8_e4m3fn_x4
E5M2 = mybir.dt.float8_e5m2_x4
E2M1 = mybir.dt.float4_e2m1fn_x4
ALU = mybir.AluOpType
ACT = mybir.ActivationFunctionType

P = 128
PACK = 4
PASSES = K // (P * PACK)
PLANES = PASSES * PACK
TILES = J // P
QUADS = 4
SCALE_ROWS = 4
PER_COLUMN = 16
BLOCK = 8
LEAD = BLOCK
ROW = LEAD + J
PAIR = 2


def tile_list_steps_timestable_rowpeaks_kernel(
    tc, xf, fk, w_words, w_scales, tb, wb_words, wb_scales, rs, offs, offs2, out
):
    nc = tc.nc
    with ExitStack() as ctx:
        lists = ctx.enter_context(tc.tile_pool(name="lists", bufs=1))
        sb = ctx.enter_context(tc.tile_pool(name="sb", bufs=1))
        ps = ctx.enter_context(tc.psum_pool(name="ps", bufs=1))

        idx = lists.tile([P, J // PER_COLUMN], U16, name="idx")
        idx2 = lists.tile([P, J // PER_COLUMN], U16, name="idx2")
        x = [sb.tile([P, T], F32, name=f"x{q}") for q in range(PLANES)]
        tb_early = [sb.tile([P, V], F32, name=f"tb{t}") for t in range(PACK // 2)]
        tb_late = sb.tile([P, 2 * V], F32, name="tb_late")
        tb_plane = [tb_early[0][:], tb_early[1][:], tb_late[:, :V], tb_late[:, V:]]
        factor = sb.tile([P, PASSES, BLOCK], F32, name="factor")
        zero = sb.tile([P, PLANES], F32, name="zero")
        xg = sb.tile([P, PLANES * ROW], F32, name="xg")
        steps = [sb.tile([P, PACK * J], F32, name=f"steps{z}") for z in range(PASSES)]
        u0 = sb.tile([P, PACK * J], BF16, name="u0", align_bytes=64)
        u0_codes = sb.tile([P, J], U32, name="u0_codes", align_bytes=64)
        u0_scales = sb.tile([P, J], U8, name="u0_scales", align_bytes=64)
        u1 = [sb.tile([P, PACK * P], BF16, name=f"u1_{jt}", align_bytes=64) for jt in range(TILES)]
        u1_codes = [sb.tile([P, P], U32, name=f"u1_codes{jt}", align_bytes=64) for jt in range(TILES)]
        u1_scales = [sb.tile([P, P], U8, name=f"u1_scales{jt}", align_bytes=64) for jt in range(TILES)]
        w_raw = [sb.tile([P, R], U32, name=f"w_raw{z}") for z in range(PASSES)]
        w_codes = [sb.tile([P, R], U32, name=f"w_codes{z}", align_bytes=64) for z in range(PASSES)]
        ws_raw = sb.tile([P, PASSES * R], U8, name="ws_raw")
        ws = sb.tile([P, PASSES * R], U8, name="ws", align_bytes=64)
        wb_codes = sb.tile([P, 2 * N], U8, name="wb_codes", align_bytes=64)
        wbs = sb.tile([P, N], U8, name="wbs", align_bytes=64)
        tg = sb.tile([P, PACK * J], F32, name="tg")
        rs_raw = sb.tile([P, TILES * N], F32, name="rs_raw")
        a = [ps.tile([P, PACK * P], F32, name=f"a{jt}") for jt in range(TILES)]
        prod = [ps.tile([P, N], F32, name=f"prod{jt}") for jt in range(TILES)]

        x_rows = xf.rearrange("(z p t) c -> z t p c", p=P, t=PACK)
        tb_rows = tb.rearrange("(p t) c -> t p c", t=PACK)

        def load_x(q):
            nc.sync.dma_start(x[q][:], x_rows[q // PACK, q % PACK])

        def scale_rows(plane, quad):
            return plane[32 * quad : 32 * quad + SCALE_ROWS, :].bitcast(I32)

        def gather_x(q):
            first = q * ROW + LEAD
            nc.scalar.activation(xg[:, first : first + J], x[q][:].indirect(idx[:]), ACT.Copy)

        def gather_tb(t, j0, j1):
            entries = idx2[:, j0 // PER_COLUMN : j1 // PER_COLUMN]
            nc.scalar.activation(tg[:, t * J + j0 : t * J + j1], tb_plane[t].indirect(entries), ACT.Copy)

        def step(q):
            z, t = divmod(q, PACK)
            first = q * ROW + LEAD
            nc.vector.scalar_tensor_tensor(
                steps[z][:, t * J : (t + 1) * J],
                xg[:, first - 1 : first + J - 1],
                -0.6,
                xg[:, first : first + J],
                ALU.mult,
                ALU.add,
            )

        def scale(dst, z, j0, j1):
            nc.vector.tensor_tensor(
                dst.rearrange("p (c i t) -> p c t i", i=PAIR, t=PACK),
                steps[z][:].rearrange("p (t c i) -> p c t i", i=PAIR, t=PACK)[:, j0 // PAIR : j1 // PAIR],
                factor[:, z, :PACK]
                .rearrange("p (c t i) -> p c t i", c=1, i=1)
                .to_broadcast([P, (j1 - j0) // PAIR, PACK, PAIR]),
                ALU.mult,
            )

        def order_w(copy, z):
            copy(
                w_codes[z][:].rearrange("p (t m) -> p m t", t=PACK),
                w_raw[z][:].rearrange("p (m t) -> p m t", t=PACK),
            )

        def first_product(z, jt, codes, scales):
            for t in range(PACK):
                nc.tensor.matmul_mx(
                    a[jt][:, t * P : (t + 1) * P],
                    lhsT=w_codes[z][:, t * P : (t + 1) * P].bitcast(E5M2),
                    lhsT_scale=ws[:, z * R + t * P : z * R + (t + 1) * P],
                    rhs=codes.bitcast(E4M3),
                    rhs_scale=scales,
                    start=(z == 0 and t == 0),
                    stop=(z == PASSES - 1 and t == PACK - 1),
                )

        nc.gpsimd.memset(ws_raw[:].bitcast(U32), 0)
        nc.gpsimd.memset(zero[:], 0.0)
        nc.gpsimd.memset(wbs[:].bitcast(U32), 0)
        nc.scalar.activation(xg[:, LEAD - 1 :: ROW], zero[:], ACT.Copy)

        nc.sync.dma_start(idx[:], offs)
        load_x(0)
        for quad in range(QUADS):
            nc.sync.dma_start(
                scale_rows(ws_raw, quad).rearrange("p (z c) -> p z c", z=PASSES),
                w_scales[:, SCALE_ROWS * quad : SCALE_ROWS * (quad + 1), :].bitcast(I32).rearrange("z r c -> r z c"),
            )
        for q in range(1, PACK):
            load_x(q)
        nc.sync.dma_start(factor[:, :, :PACK], fk.rearrange("(z p t) o -> p z (t o)", p=P, t=PACK))
        nc.sync.dma_start(idx2[:], offs2)
        for q in range(PACK, PLANES):
            load_x(q)
        for z in range(PASSES):
            nc.sync.dma_start(w_raw[z][:].bitcast(I32), w_words[z].rearrange("p c r -> p (c r)").bitcast(I32))
        for t in range(PACK // 2):
            nc.sync.dma_start(tb_plane[t], tb_rows[t])
        nc.sync.dma_start(tb_late[:], tb.rearrange("(p h t) c -> h p (t c)", h=2, t=2)[1])
        nc.sync.dma_start(wb_codes[:], wb_words[0])
        nc.sync.dma_start(rs_raw[:].rearrange("p (j n) -> p j n", j=TILES), rs.rearrange("(j p) n -> p j n", p=P))
        for quad in range(QUADS):
            nc.sync.dma_start(
                scale_rows(wbs, quad), wb_scales[0, SCALE_ROWS * quad : SCALE_ROWS * (quad + 1), :].bitcast(I32)
            )

        nc.vector.tensor_copy(
            ws[:].rearrange("p (z t m) -> p z t m", z=PASSES, t=PACK),
            ws_raw[:].rearrange("p (z m t) -> p z t m", z=PASSES, t=PACK),
        )

        for q in range(PACK):
            gather_x(q)
            step(q)
        scale(u0[:], 0, 0, J)
        gather_x(PACK)
        step(PACK)
        nc.vector.quantize_mx(u0_codes[:].bitcast(E4M3), u0_scales[:], u0[:])
        for q in range(PACK + 1, PLANES):
            gather_x(q)
            step(q)

        order_w(nc.scalar.copy, 0)
        order_w(nc.vector.tensor_copy, 1)
        for jt in range(TILES):
            slots = slice(jt * P, (jt + 1) * P)
            first_product(0, jt, u0_codes[:, slots], u0_scales[:, slots])

        def quantize_u1(jt):
            nc.vector.quantize_mx(u1_codes[jt][:].bitcast(E4M3), u1_scales[jt][:], u1[jt][:])
            first_product(1, jt, u1_codes[jt][:], u1_scales[jt][:])

        scale(u1[0][:], 1, 0, P)
        for jt in range(1, TILES):
            scale(u1[jt][:], 1, jt * P, (jt + 1) * P)
            quantize_u1(jt - 1)
        quantize_u1(TILES - 1)

        for t in range(PACK // 2):
            gather_tb(t, 0, J)
        for jt in range(TILES):
            for t in range(PACK // 2, PACK):
                gather_tb(t, jt * P, (jt + 1) * P)

        hid = [sb.tile([P, PACK * P], BF16, name=f"hid{jt}", align_bytes=64) for jt in range(TILES)]
        hid_codes = [sb.tile([P, P], U32, name=f"hid_codes{jt}", align_bytes=64) for jt in range(TILES)]
        hid_scales = [sb.tile([P, P], U8, name=f"hid_scales{jt}", align_bytes=64) for jt in range(TILES)]
        res = [sb.tile([P, N], F32, name=f"res{jt}") for jt in range(TILES)]
        mag = [sb.tile([P, N], F32, name=f"mag{jt}") for jt in range(TILES)]
        den = [sb.tile([P, 1], F32, name=f"den{jt}") for jt in range(TILES)]
        inv = [sb.tile([P, 1], F32, name=f"inv{jt}") for jt in range(TILES)]
        scaled = sb.tile([P, N], F32, name="scaled")
        y = [sb.tile([P, N], F32, name=f"y{jt}") for jt in range(TILES)]

        def hidden(jt):
            nc.vector.scalar_tensor_tensor(
                hid[jt][:].rearrange("p (j t) -> p j t", t=PACK),
                a[jt][:].rearrange("p (t j) -> p j t", t=PACK),
                0.0,
                tg[:].rearrange("p (t j) -> p j t", t=PACK)[:, jt * P : (jt + 1) * P, :],
                ALU.max,
                ALU.mult,
            )

        def second_product(jt):
            nc.vector.quantize_mx(hid_codes[jt][:].bitcast(E4M3), hid_scales[jt][:], hid[jt][:])
            nc.tensor.matmul_mx(
                prod[jt][:],
                lhsT=hid_codes[jt][:].bitcast(E4M3),
                lhsT_scale=hid_scales[jt][:],
                rhs=wb_codes[:].bitcast(E2M1),
                rhs_scale=wbs[:],
                start=True,
                stop=True,
            )
            nc.scalar.activation(mag[jt][:], prod[jt][:], ACT.Abs)

        def peak(jt):
            nc.vector.tensor_scalar(mag[jt][:], mag[jt][:], 0.2, None, ALU.add, ALU.max, accum_out=den[jt][:])

        def invert(jt):
            nc.vector.reciprocal(inv[jt][:], den[jt][:])

        def finish(jt):
            nc.vector.scalar_tensor_tensor(y[jt][:], prod[jt][:], inv[jt][:], res[jt][:], ALU.mult, ALU.add)
            nc.sync.dma_start(out[jt * P : (jt + 1) * P, :], y[jt][:])

        def finish_beside_vector(jt):
            nc.scalar.activation(scaled[:], prod[jt][:], ACT.Copy, scale=inv[jt][:])
            nc.gpsimd.tensor_tensor(y[jt][:], scaled[:], res[jt][:], ALU.add)
            nc.sync.dma_start(out[jt * P : (jt + 1) * P, :], y[jt][:])

        for jt in range(TILES):
            nc.scalar.activation(res[jt][:], rs_raw[:, jt * N : (jt + 1) * N], ACT.Copy, scale=0.3)

        hidden(0)
        hidden(1)
        second_product(0)
        hidden(2)
        second_product(1)
        peak(0)
        second_product(2)
        invert(0)
        peak(1)
        finish_beside_vector(0)
        invert(1)
        peak(2)
        finish(1)
        invert(2)
        finish(2)
